import numpy as np
import ml_dtypes


def mxq(x, axis, fmt="e4m3"):
    dtype, down = {"e4m3": (ml_dtypes.float8_e4m3fn, 7), "e5m2": (ml_dtypes.float8_e5m2, 14)}[fmt]
    v = np.moveaxis(np.asarray(x, np.float32).astype(ml_dtypes.bfloat16).astype(np.float64), axis, -1)
    blocks = v.reshape(v.shape[:-1] + (-1, 32))
    amax = np.abs(blocks).max(-1, keepdims=True)
    byte = np.maximum(np.where(amax > 0, np.frexp(amax)[1] - 1 + 127, 0) - down, 1)
    scale = np.exp2(byte - 127.0)
    codes = (blocks / scale).astype(np.float32).astype(dtype).astype(np.float64)
    return np.moveaxis((codes * scale).reshape(v.shape), -1, axis)


WIDE = False


def mx_kscale(k, group=512):
    if not WIDE:
        return np.ones(k)
    levels = np.array([18, -18])
    if group != 512:
        return np.exp2(np.random.permutation(np.resize(levels, k // group))).repeat(group)
    if k % 512:
        return np.exp2(np.random.permutation(np.resize(levels, k // 32))).repeat(32)
    a = np.empty((k // 512, 16))
    for p in range(k // 512):
        a[p, :8] = np.random.permutation(np.resize(levels, 8))
        for g in range(8):
            far = levels[np.abs(levels - a[p, g]) >= 10]
            a[p, g + 8] = far[np.random.randint(len(far))]
    return np.exp2(a.ravel()).repeat(32)


def f64(x):
    return np.asarray(x).astype(np.float64)


E2M1 = np.array([0.0, 0.5, 1.0, 1.5, 2.0, 3.0, 4.0, 6.0, -0.0, -0.5, -1.0, -1.5, -2.0, -3.0, -4.0, -6.0])


def pack_group(w):
    k, n = w.shape
    w = f64(np.asarray(w, np.float32).astype(ml_dtypes.bfloat16)).reshape(k // 32, 32, n)
    amax = np.abs(w).max(1)
    mant, ex = np.frexp(amax / 6.0)
    byte = np.clip(np.where(amax > 0, np.where(mant > 0.5, ex, ex - 1) + 127, 1), 1, 254)
    scaled = (w * np.exp2(127.0 - byte)[:, None, :]).reshape(k, n).astype(np.float32)
    c = np.ascontiguousarray(scaled.reshape(k // 4, 4, n).transpose(0, 2, 1)).astype(ml_dtypes.float4_e2m1fn).view(np.uint8) & 0xF
    return np.ascontiguousarray((c[..., 0::2] | (c[..., 1::2] << 4)).reshape(k // 4, 2 * n)), byte.astype(np.uint8)


def unpack_group(words, scales):
    p, n = words.shape[0], scales.shape[1]
    words = np.ascontiguousarray(words).reshape(p, n, 2)
    nib = np.empty((p, n, 4), np.uint8)
    nib[..., 0::2] = words & 0xF
    nib[..., 1::2] = words >> 4
    return E2M1[nib].transpose(0, 2, 1).reshape(4 * p, n) * np.repeat(np.exp2(scales.astype(np.float64) - 127.0), 32, axis=0)


G, D, M, N = 4, 128, 256, 1024


def setup_inputs():
    n = np.random.standard_normal
    s = mx_kscale(D, 0)[:, None]
    w_ = [pack_group(w) for w in n((G, D, M)) / np.sqrt(D) / s]
    return {
        "x": (n((G, D, N)) * s).astype(np.float32),
        "w_words": np.stack([w[0] for w in w_]),
        "w_scales": np.stack([w[1] for w in w_]),
        "r": n((G, M, N)).astype(np.float32),
    }


def reference(x, w_words, w_scales, r):
    xq = mxq(f64(x), 1, "e4m3")
    y = np.stack([unpack_group(w_words[g], w_scales[g]) for g in range(G)]).transpose(0, 2, 1) @ xq
    y = np.maximum(y, 0.0)
    y = y + f64(r)
    return y

@@ -1,0 +1,131 @@
+from contextlib import ExitStack
+
+import concourse.mybir as mybir
+
+G, D, M, N = 4, 128, 256, 1024
+FLOPS = 2 * G * D * M * N
+
+F32 = mybir.dt.float32
+BF16 = mybir.dt.bfloat16
+I32 = mybir.dt.int32
+U32 = mybir.dt.uint32
+U8 = mybir.dt.uint8
+FP8X4 = mybir.dt.float8_e4m3fn_x4
+FP4X4 = mybir.dt.float4_e2m1fn_x4
+ALU = mybir.AluOpType
+
+P = 128
+PACK = 4
+ROWS = D // PACK
+SCALE_ROWS = D // 32
+SLOTS = M // P
+N_TILE = 512
+VECTOR_COLS = 608
+
+
+def tile_rows_glin_relu_res_kernel(tc, x, w_words, w_scales, r, out):
+    nc = tc.nc
+    with ExitStack() as ctx:
+        sb = ctx.enter_context(tc.tile_pool(name="sb", bufs=1))
+        ps = ctx.enter_context(tc.psum_pool(name="ps", bufs=1))
+        ctx.enter_context(tc.manual_schedule())
+
+        x_raw = sb.tile([P, PACK, N], F32, name="x_raw")
+        x_bf = sb.tile([P, N, PACK], BF16, name="x_bf", align_bytes=64)
+        x_codes = sb.tile([P, N], U32, name="x_codes", align_bytes=64)
+        x_scales = sb.tile([P, N], U8, name="x_scales", align_bytes=64)
+        w_raw = sb.tile([P, 2 * M], U8, name="w_raw", align_bytes=64)
+        ws_raw = sb.tile([P, M], U8, name="ws_raw", align_bytes=64)
+        w_codes = sb.tile([P, 2 * M], U8, name="w_codes", align_bytes=64)
+        ws = sb.tile([P, M], U8, name="ws", align_bytes=64)
+        res = [sb.tile([P, SLOTS, N], F32, name="res%d" % g) for g in range(G)]
+        y = [sb.tile([P, SLOTS, N], F32, name="y%d" % g) for g in range(G)]
+        acc = [[ps.tile([P, N_TILE], F32, name="acc%d_%d" % (g, h)) for h in range(SLOTS)] for g in range(G)]
+
+        nc.sync.dma_start(
+            out=x_raw[:].rearrange("p j n -> p (j n)"),
+            in_=x.rearrange("g (p j) n -> (g p) (j n)", j=PACK),
+        )
+        for g in range(G):
+            nc.sync.dma_start(
+                out=res[g][:].rearrange("p h n -> p (h n)"),
+                in_=r[g].rearrange("(p h) n -> p (h n)", h=SLOTS),
+            )
+
+        nc.vector.memset(ws_raw[:].bitcast(I32), 0)
+        nc.scalar.dma_start(out=w_raw[:].bitcast(I32), in_=w_words.rearrange("g p b -> (g p) b").bitcast(I32))
+        for g in range(G):
+            queue = nc.scalar if g < G // 2 else nc.gpsimd
+            queue.dma_start(
+                out=ws_raw[ROWS * g : ROWS * g + SCALE_ROWS, :].bitcast(I32), in_=w_scales[g].bitcast(I32)
+            )
+
+        nc.vector.tensor_copy(
+            out=w_codes[:].rearrange("p (h q b) -> p q h b", h=SLOTS, b=2),
+            in_=w_raw[:].rearrange("p (q h b) -> p q h b", h=SLOTS, b=2),
+        )
+        nc.vector.tensor_copy(
+            out=ws[:].rearrange("p (h q) -> p q h", h=SLOTS),
+            in_=ws_raw[:].rearrange("p (q h) -> p q h", h=SLOTS),
+        )
+
+        def interleave(copy, first, last):
+            copy(
+                out=x_bf[:, first:last, :].rearrange("p (c i) j -> p c j i", i=4),
+                in_=x_raw[:, :, first:last].rearrange("p j (c i) -> p c j i", i=4),
+            )
+
+        def quantize(t):
+            cols = slice(t * N_TILE, (t + 1) * N_TILE)
+            nc.vector.quantize_mx(
+                out=x_codes[:, cols].bitcast(FP8X4),
+                scales=x_scales[:, cols],
+                in_=x_bf[:, cols, :].rearrange("p n j -> p (n j)"),
+            )
+
+        def multiply(g, h, t):
+            rows = slice(ROWS * g, ROWS * (g + 1))
+            cols = slice(t * N_TILE, (t + 1) * N_TILE)
+            nc.tensor.matmul_mx(
+                out=acc[g][h][:],
+                lhsT=w_codes[rows, 2 * P * h : 2 * P * (h + 1)].bitcast(FP4X4),
+                lhsT_scale=ws[rows, P * h : P * (h + 1)],
+                rhs=x_codes[rows, cols].bitcast(FP8X4),
+                rhs_scale=x_scales[rows, cols],
+                start=True,
+                stop=True,
+            )
+
+        def finish(g, h, t):
+            cols = slice(t * N_TILE, (t + 1) * N_TILE)
+            nc.vector.scalar_tensor_tensor(
+                out=y[g][:, h, cols],
+                in0=acc[g][h][:],
+                scalar=0.0,
+                in1=res[g][:, h, cols],
+                op0=ALU.max,
+                op1=ALU.add,
+            )
+            if t == 0:
+                multiply(g, h, 1)
+
+        interleave(nc.scalar.copy, VECTOR_COLS, N)
+        interleave(nc.vector.tensor_copy, 0, N_TILE)
+        interleave(nc.vector.tensor_copy, N_TILE, VECTOR_COLS)
+        quantize(0)
+        quantize(1)
+        for h in range(SLOTS):
+            for g in range(G):
+                multiply(g, h, 0)
+
+        finish(0, 0, 0)
+        for g in range(G):
+            finish(g, 1, 0)
+            if g + 1 < G:
+                finish(g + 1, 0, 0)
+            finish(g, 0, 1)
+            finish(g, 1, 1)
+            nc.sync.dma_start(
+                out=out[g].rearrange("(p h) n -> p (h n)", h=SLOTS),
+                in_=y[g][:].rearrange("p h n -> p (h n)"),
+            )

@@ -55,8 +55,7 @@ def tile_rows_glin_relu_res_kernel(tc, x, w_words, w_scales, r, out):
         nc.vector.memset(ws_raw[:].bitcast(I32), 0)
         nc.scalar.dma_start(out=w_raw[:].bitcast(I32), in_=w_words.rearrange("g p b -> (g p) b").bitcast(I32))
         for g in range(G):
-            queue = nc.scalar if g < G // 2 else nc.gpsimd
-            queue.dma_start(
+            nc.scalar.dma_start(
                 out=ws_raw[ROWS * g : ROWS * g + SCALE_ROWS, :].bitcast(I32), in_=w_scales[g].bitcast(I32)
             )
 
@@ -106,26 +105,27 @@ def tile_rows_glin_relu_res_kernel(tc, x, w_words, w_scales, r, out):
                 op0=ALU.max,
                 op1=ALU.add,
             )
-            if t == 0:
-                multiply(g, h, 1)
 
         interleave(nc.scalar.copy, VECTOR_COLS, N)
         interleave(nc.vector.tensor_copy, 0, N_TILE)
         interleave(nc.vector.tensor_copy, N_TILE, VECTOR_COLS)
         quantize(0)
         quantize(1)
-        for h in range(SLOTS):
-            for g in range(G):
-                multiply(g, h, 0)
-
-        finish(0, 0, 0)
+        order = [(0, 0, 0)]
         for g in range(G):
-            finish(g, 1, 0)
+            order.append((g, 1, 0))
             if g + 1 < G:
-                finish(g + 1, 0, 0)
-            finish(g, 0, 1)
-            finish(g, 1, 1)
-            nc.sync.dma_start(
-                out=out[g].rearrange("(p h) n -> p (h n)", h=SLOTS),
-                in_=y[g][:].rearrange("p h n -> p (h n)"),
-            )
+                order.append((g + 1, 0, 0))
+            order.extend([(g, 0, 1), (g, 1, 1)])
+
+        multiply(*order[0])
+        multiply(*order[1])
+        for i, (g, h, t) in enumerate(order):
+            finish(g, h, t)
+            if i + 2 < len(order):
+                multiply(*order[i + 2])
+            if (h, t) == (1, 1):
+                nc.sync.dma_start(
+                    out=out[g].rearrange("(p h) n -> p (h n)", h=SLOTS),
+                    in_=y[g][:].rearrange("p h n -> p (h n)"),
+                )

@@ -46,26 +46,21 @@ def tile_rows_glin_relu_res_kernel(tc, x, w_words, w_scales, r, out):
             out=x_raw[:].rearrange("p j n -> p (j n)"),
             in_=x.rearrange("g (p j) n -> (g p) (j n)", j=PACK),
         )
+        nc.vector.memset(ws_raw[:].bitcast(I32), 0)
+        nc.scalar.dma_start(out=w_raw[:].bitcast(I32), in_=w_words.rearrange("g p b -> (g p) b").bitcast(I32))
+        for g in range(G):
+            nc.sync.dma_start(
+                out=ws_raw[ROWS * g : ROWS * g + SCALE_ROWS, :].bitcast(I32), in_=w_scales[g].bitcast(I32)
+            )
         for g in range(G):
             nc.sync.dma_start(
                 out=res[g][:].rearrange("p h n -> p (h n)"),
                 in_=r[g].rearrange("(p h) n -> p (h n)", h=SLOTS),
             )
 
-        nc.vector.memset(ws_raw[:].bitcast(I32), 0)
-        nc.scalar.dma_start(out=w_raw[:].bitcast(I32), in_=w_words.rearrange("g p b -> (g p) b").bitcast(I32))
-        for g in range(G):
-            nc.scalar.dma_start(
-                out=ws_raw[ROWS * g : ROWS * g + SCALE_ROWS, :].bitcast(I32), in_=w_scales[g].bitcast(I32)
-            )
-
         nc.vector.tensor_copy(
             out=w_codes[:].rearrange("p (h q b) -> p q h b", h=SLOTS, b=2),
             in_=w_raw[:].rearrange("p (q h b) -> p q h b", h=SLOTS, b=2),
-        )
-        nc.vector.tensor_copy(
-            out=ws[:].rearrange("p (h q) -> p q h", h=SLOTS),
-            in_=ws_raw[:].rearrange("p (q h) -> p q h", h=SLOTS),
         )
 
         def interleave(copy, first, last):
@@ -110,6 +105,10 @@ def tile_rows_glin_relu_res_kernel(tc, x, w_words, w_scales, r, out):
         interleave(nc.vector.tensor_copy, 0, N_TILE)
         interleave(nc.vector.tensor_copy, N_TILE, VECTOR_COLS)
         quantize(0)
+        nc.vector.tensor_copy(
+            out=ws[:].rearrange("p (h q) -> p q h", h=SLOTS),
+            in_=ws_raw[:].rearrange("p (q h) -> p q h", h=SLOTS),
+        )
         quantize(1)
         order = [(0, 0, 0)]
         for g in range(G):
@@ -124,7 +123,9 @@ def tile_rows_glin_relu_res_kernel(tc, x, w_words, w_scales, r, out):
             finish(g, h, t)
             if i + 2 < len(order):
                 multiply(*order[i + 2])
-            if (h, t) == (1, 1):
+            if g == G - 1 and t == 1:
+                nc.sync.dma_start(out=out[g].rearrange("(p h) n -> p h n", h=SLOTS)[:, h, :], in_=y[g][:, h, :])
+            elif (h, t) == (1, 1):
                 nc.sync.dma_start(
                     out=out[g].rearrange("(p h) n -> p (h n)", h=SLOTS),
                     in_=y[g][:].rearrange("p h n -> p (h n)"),

@@ -21,6 +21,7 @@ SCALE_ROWS = D // 32
 SLOTS = M // P
 N_TILE = 512
 VECTOR_COLS = 608
+DMA_ALIGN = 256
 
 
 def tile_rows_glin_relu_res_kernel(tc, x, w_words, w_scales, r, out):
@@ -30,16 +31,16 @@ def tile_rows_glin_relu_res_kernel(tc, x, w_words, w_scales, r, out):
         ps = ctx.enter_context(tc.psum_pool(name="ps", bufs=1))
         ctx.enter_context(tc.manual_schedule())
 
-        x_raw = sb.tile([P, PACK, N], F32, name="x_raw")
+        x_raw = sb.tile([P, PACK, N], F32, name="x_raw", align_bytes=DMA_ALIGN)
         x_bf = sb.tile([P, N, PACK], BF16, name="x_bf", align_bytes=64)
         x_codes = sb.tile([P, N], U32, name="x_codes", align_bytes=64)
         x_scales = sb.tile([P, N], U8, name="x_scales", align_bytes=64)
-        w_raw = sb.tile([P, 2 * M], U8, name="w_raw", align_bytes=64)
-        ws_raw = sb.tile([P, M], U8, name="ws_raw", align_bytes=64)
+        w_raw = sb.tile([P, 2 * M], U8, name="w_raw", align_bytes=DMA_ALIGN)
+        ws_raw = sb.tile([P, M], U8, name="ws_raw", align_bytes=DMA_ALIGN)
         w_codes = sb.tile([P, 2 * M], U8, name="w_codes", align_bytes=64)
         ws = sb.tile([P, M], U8, name="ws", align_bytes=64)
-        res = [sb.tile([P, SLOTS, N], F32, name="res%d" % g) for g in range(G)]
-        y = [sb.tile([P, SLOTS, N], F32, name="y%d" % g) for g in range(G)]
+        res = [sb.tile([P, SLOTS, N], F32, name="res%d" % g, align_bytes=DMA_ALIGN) for g in range(G)]
+        y = [sb.tile([P, SLOTS, N], F32, name="y%d" % g, align_bytes=DMA_ALIGN) for g in range(G)]
         acc = [[ps.tile([P, N_TILE], F32, name="acc%d_%d" % (g, h)) for h in range(SLOTS)] for g in range(G)]
 
         nc.sync.dma_start(

@@ -124,9 +124,7 @@ def tile_rows_glin_relu_res_kernel(tc, x, w_words, w_scales, r, out):
             finish(g, h, t)
             if i + 2 < len(order):
                 multiply(*order[i + 2])
-            if g == G - 1 and t == 1:
-                nc.sync.dma_start(out=out[g].rearrange("(p h) n -> p h n", h=SLOTS)[:, h, :], in_=y[g][:, h, :])
-            elif (h, t) == (1, 1):
+            if (h, t) == (1, 1):
                 nc.sync.dma_start(
                     out=out[g].rearrange("(p h) n -> p (h n)", h=SLOTS),
                     in_=y[g][:].rearrange("p h n -> p (h n)"),

@@ -13,6 +13,7 @@ U8 = mybir.dt.uint8
 FP8X4 = mybir.dt.float8_e4m3fn_x4
 FP4X4 = mybir.dt.float4_e2m1fn_x4
 ALU = mybir.AluOpType
+ACT = mybir.ActivationFunctionType
 
 P = 128
 PACK = 4
@@ -20,7 +21,7 @@ ROWS = D // PACK
 SCALE_ROWS = D // 32
 SLOTS = M // P
 N_TILE = 512
-VECTOR_COLS = 608
+VECTOR_COLS = (304, 256)
 DMA_ALIGN = 256
 
 
@@ -102,30 +103,45 @@ def tile_rows_glin_relu_res_kernel(tc, x, w_words, w_scales, r, out):
                 op1=ALU.add,
             )
 
-        interleave(nc.scalar.copy, VECTOR_COLS, N)
-        interleave(nc.vector.tensor_copy, 0, N_TILE)
-        interleave(nc.vector.tensor_copy, N_TILE, VECTOR_COLS)
-        quantize(0)
-        nc.vector.tensor_copy(
-            out=ws[:].rearrange("p (h q) -> p q h", h=SLOTS),
-            in_=ws_raw[:].rearrange("p (q h) -> p q h", h=SLOTS),
-        )
-        quantize(1)
+        for t, share in enumerate(VECTOR_COLS):
+            first = t * N_TILE
+            interleave(nc.scalar.copy, first + share, first + N_TILE)
+            interleave(nc.vector.tensor_copy, first, first + share)
+            if t == 0:
+                nc.vector.tensor_copy(
+                    out=ws[:].rearrange("p (h q) -> p q h", h=SLOTS),
+                    in_=ws_raw[:].rearrange("p (q h) -> p q h", h=SLOTS),
+                )
+            quantize(t)
+
+        def store(g):
+            nc.sync.dma_start(
+                out=out[g].rearrange("(p h) n -> p (h n)", h=SLOTS),
+                in_=y[g][:].rearrange("p h n -> p (h n)"),
+            )
+
+        last = G - 1
         order = [(0, 0, 0)]
-        for g in range(G):
+        for g in range(last):
             order.append((g, 1, 0))
-            if g + 1 < G:
+            if g + 1 < last:
                 order.append((g + 1, 0, 0))
+            else:
+                order.append((last, 1, 0))
             order.extend([(g, 0, 1), (g, 1, 1)])
+        order.extend([(last, 0, 1), (last, 1, 1)])
 
         multiply(*order[0])
         multiply(*order[1])
+        multiply(last, 0, 0)
+        nc.scalar.activation(out=y[last][:, 0, 0:N_TILE], in_=acc[last][0][:], func=ACT.Relu)
         for i, (g, h, t) in enumerate(order):
             finish(g, h, t)
             if i + 2 < len(order):
                 multiply(*order[i + 2])
-            if (h, t) == (1, 1):
-                nc.sync.dma_start(
-                    out=out[g].rearrange("(p h) n -> p (h n)", h=SLOTS),
-                    in_=y[g][:].rearrange("p h n -> p (h n)"),
-                )
+            if (h, t) == (1, 1) and g < last:
+                store(g)
+        nc.vector.tensor_tensor(
+            out=y[last][:, 0, 0:N_TILE], in0=y[last][:, 0, 0:N_TILE], in1=res[last][:, 0, 0:N_TILE], op=ALU.add
+        )
+        store(last)

@@ -23,6 +23,7 @@ SLOTS = M // P
 N_TILE = 512
 VECTOR_COLS = (304, 256)
 DMA_ALIGN = 256
+EARLY_COLS = 512
 
 
 def tile_rows_glin_relu_res_kernel(tc, x, w_words, w_scales, r, out):
@@ -50,14 +51,19 @@ def tile_rows_glin_relu_res_kernel(tc, x, w_words, w_scales, r, out):
         )
         nc.vector.memset(ws_raw[:].bitcast(I32), 0)
         nc.scalar.dma_start(out=w_raw[:].bitcast(I32), in_=w_words.rearrange("g p b -> (g p) b").bitcast(I32))
+        nc.scalar.dma_start(
+            out=res[G - 1][:, SLOTS - 1, N - EARLY_COLS : N],
+            in_=r[G - 1].rearrange("(p h) n -> p h n", h=SLOTS)[:, SLOTS - 1, N - EARLY_COLS : N],
+        )
         for g in range(G):
             nc.sync.dma_start(
                 out=ws_raw[ROWS * g : ROWS * g + SCALE_ROWS, :].bitcast(I32), in_=w_scales[g].bitcast(I32)
             )
         for g in range(G):
+            width = SLOTS * N - (EARLY_COLS if g == G - 1 else 0)
             nc.sync.dma_start(
-                out=res[g][:].rearrange("p h n -> p (h n)"),
-                in_=r[g].rearrange("(p h) n -> p (h n)", h=SLOTS),
+                out=res[g][:].rearrange("p h n -> p (h n)")[:, 0:width],
+                in_=r[g].rearrange("(p h) n -> p (h n)", h=SLOTS)[:, 0:width],
             )
 
         nc.vector.tensor_copy(

@@ -23,6 +23,7 @@ SLOTS = M // P
 N_TILE = 512
 VECTOR_COLS = (304, 256)
 DMA_ALIGN = 256
+TAIL_COLS = 256
 EARLY_COLS = 512
 
 
@@ -150,4 +151,8 @@ def tile_rows_glin_relu_res_kernel(tc, x, w_words, w_scales, r, out):
         nc.vector.tensor_tensor(
             out=y[last][:, 0, 0:N_TILE], in0=y[last][:, 0, 0:N_TILE], in1=res[last][:, 0, 0:N_TILE], op=ALU.add
         )
-        store(last)
+        whole = out[last].rearrange("(p h) n -> p (h n)", h=SLOTS)
+        result = y[last][:].rearrange("p h n -> p (h n)")
+        cut = SLOTS * N - TAIL_COLS
+        nc.sync.dma_start(out=whole[:, 0:cut], in_=result[:, 0:cut])
+        nc.sync.dma_start(out=whole[:, cut : SLOTS * N], in_=result[:, cut : SLOTS * N])

@@ -23,6 +23,7 @@ SLOTS = M // P
 N_TILE = 512
 VECTOR_COLS = (304, 256)
 DMA_ALIGN = 256
+SPREAD = 4
 TAIL_COLS = 256
 EARLY_COLS = 512
 
@@ -54,7 +55,7 @@ def tile_rows_glin_relu_res_kernel(tc, x, w_words, w_scales, r, out):
         nc.scalar.dma_start(out=w_raw[:].bitcast(I32), in_=w_words.rearrange("g p b -> (g p) b").bitcast(I32))
         nc.scalar.dma_start(
             out=res[G - 1][:, SLOTS - 1, N - EARLY_COLS : N],
-            in_=r[G - 1].rearrange("(p h) n -> p h n", h=SLOTS)[:, SLOTS - 1, N - EARLY_COLS : N],
+            in_=r[G - 1].rearrange("(b a h) n -> a b h n", b=SPREAD, h=SLOTS)[:, :, SLOTS - 1, N - EARLY_COLS : N],
         )
         for g in range(G):
             nc.sync.dma_start(
@@ -64,12 +65,12 @@ def tile_rows_glin_relu_res_kernel(tc, x, w_words, w_scales, r, out):
             width = SLOTS * N - (EARLY_COLS if g == G - 1 else 0)
             nc.sync.dma_start(
                 out=res[g][:].rearrange("p h n -> p (h n)")[:, 0:width],
-                in_=r[g].rearrange("(p h) n -> p (h n)", h=SLOTS)[:, 0:width],
+                in_=r[g].rearrange("(b a h) n -> a b (h n)", b=SPREAD, h=SLOTS)[:, :, 0:width],
             )
 
         nc.vector.tensor_copy(
-            out=w_codes[:].rearrange("p (h q b) -> p q h b", h=SLOTS, b=2),
-            in_=w_raw[:].rearrange("p (q h b) -> p q h b", h=SLOTS, b=2),
+            out=w_codes[:].rearrange("p (h a b y) -> p b a h y", h=SLOTS, b=SPREAD, y=2),
+            in_=w_raw[:].rearrange("p (b a h y) -> p b a h y", h=SLOTS, b=SPREAD, y=2),
         )
 
         def interleave(copy, first, last):
@@ -116,14 +117,14 @@ def tile_rows_glin_relu_res_kernel(tc, x, w_words, w_scales, r, out):
             interleave(nc.vector.tensor_copy, first, first + share)
             if t == 0:
                 nc.vector.tensor_copy(
-                    out=ws[:].rearrange("p (h q) -> p q h", h=SLOTS),
-                    in_=ws_raw[:].rearrange("p (q h) -> p q h", h=SLOTS),
+                    out=ws[:].rearrange("p (h a b) -> p b a h", h=SLOTS, b=SPREAD),
+                    in_=ws_raw[:].rearrange("p (b a h) -> p b a h", h=SLOTS, b=SPREAD),
                 )
             quantize(t)
 
         def store(g):
             nc.sync.dma_start(
-                out=out[g].rearrange("(p h) n -> p (h n)", h=SLOTS),
+                out=out[g].rearrange("(b a h) n -> a b (h n)", b=SPREAD, h=SLOTS),
                 in_=y[g][:].rearrange("p h n -> p (h n)"),
             )
 
@@ -151,8 +152,8 @@ def tile_rows_glin_relu_res_kernel(tc, x, w_words, w_scales, r, out):
         nc.vector.tensor_tensor(
             out=y[last][:, 0, 0:N_TILE], in0=y[last][:, 0, 0:N_TILE], in1=res[last][:, 0, 0:N_TILE], op=ALU.add
         )
-        whole = out[last].rearrange("(p h) n -> p (h n)", h=SLOTS)
+        whole = out[last].rearrange("(b a h) n -> a b (h n)", b=SPREAD, h=SLOTS)
         result = y[last][:].rearrange("p h n -> p (h n)")
         cut = SLOTS * N - TAIL_COLS
-        nc.sync.dma_start(out=whole[:, 0:cut], in_=result[:, 0:cut])
-        nc.sync.dma_start(out=whole[:, cut : SLOTS * N], in_=result[:, cut : SLOTS * N])
+        nc.sync.dma_start(out=whole[:, :, 0:cut], in_=result[:, 0:cut])
+        nc.sync.dma_start(out=whole[:, :, cut : SLOTS * N], in_=result[:, cut : SLOTS * N])

@@ -24,8 +24,7 @@ N_TILE = 512
 VECTOR_COLS = (304, 256)
 DMA_ALIGN = 256
 SPREAD = 4
-TAIL_COLS = 256
-EARLY_COLS = 512
+WORD_PARTS = ((0, 64), (64, 96), (96, 128))
 
 
 def tile_rows_glin_relu_res_kernel(tc, x, w_words, w_scales, r, out):
@@ -40,9 +39,9 @@ def tile_rows_glin_relu_res_kernel(tc, x, w_words, w_scales, r, out):
         x_codes = sb.tile([P, N], U32, name="x_codes", align_bytes=64)
         x_scales = sb.tile([P, N], U8, name="x_scales", align_bytes=64)
         w_raw = sb.tile([P, 2 * M], U8, name="w_raw", align_bytes=DMA_ALIGN)
-        ws_raw = sb.tile([P, M], U8, name="ws_raw", align_bytes=DMA_ALIGN)
+        ws_raw = [sb.tile([P, M], U8, name="ws_raw%d" % u, align_bytes=DMA_ALIGN) for u in range(2)]
+        ws = [sb.tile([P, M], U8, name="ws%d" % u, align_bytes=64) for u in range(2)]
         w_codes = sb.tile([P, 2 * M], U8, name="w_codes", align_bytes=64)
-        ws = sb.tile([P, M], U8, name="ws", align_bytes=64)
         res = [sb.tile([P, SLOTS, N], F32, name="res%d" % g, align_bytes=DMA_ALIGN) for g in range(G)]
         y = [sb.tile([P, SLOTS, N], F32, name="y%d" % g, align_bytes=DMA_ALIGN) for g in range(G)]
         acc = [[ps.tile([P, N_TILE], F32, name="acc%d_%d" % (g, h)) for h in range(SLOTS)] for g in range(G)]
@@ -51,22 +50,30 @@ def tile_rows_glin_relu_res_kernel(tc, x, w_words, w_scales, r, out):
             out=x_raw[:].rearrange("p j n -> p (j n)"),
             in_=x.rearrange("g (p j) n -> (g p) (j n)", j=PACK),
         )
-        nc.vector.memset(ws_raw[:].bitcast(I32), 0)
-        nc.scalar.dma_start(out=w_raw[:].bitcast(I32), in_=w_words.rearrange("g p b -> (g p) b").bitcast(I32))
-        nc.scalar.dma_start(
-            out=res[G - 1][:, SLOTS - 1, N - EARLY_COLS : N],
-            in_=r[G - 1].rearrange("(b a h) n -> a b h n", b=SPREAD, h=SLOTS)[:, :, SLOTS - 1, N - EARLY_COLS : N],
-        )
-        for g in range(G):
+        for tile in ws_raw:
+            nc.vector.memset(tile[:].bitcast(I32), 0)
+        w_rows = w_words.rearrange("g p b -> (g p) b").bitcast(I32)
+        for first, end in WORD_PARTS:
+            nc.scalar.dma_start(out=w_raw[first:end, :].bitcast(I32), in_=w_rows[first:end, :])
+
+        def load_scales(g):
             nc.sync.dma_start(
-                out=ws_raw[ROWS * g : ROWS * g + SCALE_ROWS, :].bitcast(I32), in_=w_scales[g].bitcast(I32)
+                out=ws_raw[g // (G - 1)][ROWS * g : ROWS * g + SCALE_ROWS, :].bitcast(I32),
+                in_=w_scales[g].bitcast(I32),
             )
-        for g in range(G):
-            width = SLOTS * N - (EARLY_COLS if g == G - 1 else 0)
+
+        def load_residual(g):
             nc.sync.dma_start(
-                out=res[g][:].rearrange("p h n -> p (h n)")[:, 0:width],
-                in_=r[g].rearrange("(b a h) n -> a b (h n)", b=SPREAD, h=SLOTS)[:, :, 0:width],
+                out=res[g][:].rearrange("p h n -> p (h n)"),
+                in_=r[g].rearrange("(b a h) n -> a b (h n)", b=SPREAD, h=SLOTS),
             )
+
+        for g in range(G - 1):
+            load_scales(g)
+        load_residual(0)
+        load_scales(G - 1)
+        for g in range(1, G):
+            load_residual(g)
 
         nc.vector.tensor_copy(
             out=w_codes[:].rearrange("p (h a b y) -> p b a h y", h=SLOTS, b=SPREAD, y=2),
@@ -93,7 +100,7 @@ def tile_rows_glin_relu_res_kernel(tc, x, w_words, w_scales, r, out):
             nc.tensor.matmul_mx(
                 out=acc[g][h][:],
                 lhsT=w_codes[rows, 2 * P * h : 2 * P * (h + 1)].bitcast(FP4X4),
-                lhsT_scale=ws[rows, P * h : P * (h + 1)],
+                lhsT_scale=ws[g // (G - 1)][rows, P * h : P * (h + 1)],
                 rhs=x_codes[rows, cols].bitcast(FP8X4),
                 rhs_scale=x_scales[rows, cols],
                 start=True,
@@ -115,11 +122,10 @@ def tile_rows_glin_relu_res_kernel(tc, x, w_words, w_scales, r, out):
             first = t * N_TILE
             interleave(nc.scalar.copy, first + share, first + N_TILE)
             interleave(nc.vector.tensor_copy, first, first + share)
-            if t == 0:
-                nc.vector.tensor_copy(
-                    out=ws[:].rearrange("p (h a b) -> p b a h", h=SLOTS, b=SPREAD),
-                    in_=ws_raw[:].rearrange("p (b a h) -> p b a h", h=SLOTS, b=SPREAD),
-                )
+            nc.vector.tensor_copy(
+                out=ws[t][:].rearrange("p (h a b) -> p b a h", h=SLOTS, b=SPREAD),
+                in_=ws_raw[t][:].rearrange("p (b a h) -> p b a h", h=SLOTS, b=SPREAD),
+            )
             quantize(t)
 
         def store(g):
@@ -149,11 +155,8 @@ def tile_rows_glin_relu_res_kernel(tc, x, w_words, w_scales, r, out):
                 multiply(*order[i + 2])
             if (h, t) == (1, 1) and g < last:
                 store(g)
-        nc.vector.tensor_tensor(
-            out=y[last][:, 0, 0:N_TILE], in0=y[last][:, 0, 0:N_TILE], in1=res[last][:, 0, 0:N_TILE], op=ALU.add
-        )
-        whole = out[last].rearrange("(b a h) n -> a b (h n)", b=SPREAD, h=SLOTS)
-        result = y[last][:].rearrange("p h n -> p (h n)")
-        cut = SLOTS * N - TAIL_COLS
-        nc.sync.dma_start(out=whole[:, :, 0:cut], in_=result[:, 0:cut])
-        nc.sync.dma_start(out=whole[:, :, cut : SLOTS * N], in_=result[:, cut : SLOTS * N])
+            if (g, h, t) == (last - 1, 1, 1):
+                nc.vector.tensor_tensor(
+                    out=y[last][:, 0, 0:N_TILE], in0=y[last][:, 0, 0:N_TILE], in1=res[last][:, 0, 0:N_TILE], op=ALU.add
+                )
+        store(last)

@@ -21,7 +21,7 @@ ROWS = D // PACK
 SCALE_ROWS = D // 32
 SLOTS = M // P
 N_TILE = 512
-VECTOR_COLS = (304, 256)
+VECTOR_COLS = (256, 224)
 DMA_ALIGN = 256
 SPREAD = 4
 WORD_PARTS = ((0, 64), (64, 96), (96, 128))
@@ -54,7 +54,7 @@ def tile_rows_glin_relu_res_kernel(tc, x, w_words, w_scales, r, out):
             nc.vector.memset(tile[:].bitcast(I32), 0)
         w_rows = w_words.rearrange("g p b -> (g p) b").bitcast(I32)
         for first, end in WORD_PARTS:
-            nc.scalar.dma_start(out=w_raw[first:end, :].bitcast(I32), in_=w_rows[first:end, :])
+            nc.sync.dma_start(out=w_raw[first:end, :].bitcast(I32), in_=w_rows[first:end, :])
 
         def load_scales(g):
             nc.sync.dma_start(
@@ -74,11 +74,6 @@ def tile_rows_glin_relu_res_kernel(tc, x, w_words, w_scales, r, out):
         load_scales(G - 1)
         for g in range(1, G):
             load_residual(g)
-
-        nc.vector.tensor_copy(
-            out=w_codes[:].rearrange("p (h a b y) -> p b a h y", h=SLOTS, b=SPREAD, y=2),
-            in_=w_raw[:].rearrange("p (b a h y) -> p b a h y", h=SLOTS, b=SPREAD, y=2),
-        )
 
         def interleave(copy, first, last):
             copy(
@@ -122,9 +117,14 @@ def tile_rows_glin_relu_res_kernel(tc, x, w_words, w_scales, r, out):
             first = t * N_TILE
             interleave(nc.scalar.copy, first + share, first + N_TILE)
             interleave(nc.vector.tensor_copy, first, first + share)
+            if t == 0:
+                nc.vector.tensor_copy(
+                    out=w_codes[:].rearrange("p (h a b y) -> p h a b y", h=SLOTS, b=SPREAD, y=2),
+                    in_=w_raw[:].rearrange("p (b a h y) -> p h a b y", h=SLOTS, b=SPREAD, y=2),
+                )
             nc.vector.tensor_copy(
-                out=ws[t][:].rearrange("p (h a b) -> p b a h", h=SLOTS, b=SPREAD),
-                in_=ws_raw[t][:].rearrange("p (b a h) -> p b a h", h=SLOTS, b=SPREAD),
+                out=ws[t][:].rearrange("p (h a b) -> p h a b", h=SLOTS, b=SPREAD),
+                in_=ws_raw[t][:].rearrange("p (b a h) -> p h a b", h=SLOTS, b=SPREAD),
             )
             quantize(t)
 

@@ -21,10 +21,9 @@ ROWS = D // PACK
 SCALE_ROWS = D // 32
 SLOTS = M // P
 N_TILE = 512
-VECTOR_COLS = (256, 224)
+VECTOR_COLS = (320, 128)
 DMA_ALIGN = 256
 SPREAD = 4
-WORD_PARTS = ((0, 64), (64, 96), (96, 128))
 
 
 def tile_rows_glin_relu_res_kernel(tc, x, w_words, w_scales, r, out):
@@ -39,46 +38,36 @@ def tile_rows_glin_relu_res_kernel(tc, x, w_words, w_scales, r, out):
         x_codes = sb.tile([P, N], U32, name="x_codes", align_bytes=64)
         x_scales = sb.tile([P, N], U8, name="x_scales", align_bytes=64)
         w_raw = sb.tile([P, 2 * M], U8, name="w_raw", align_bytes=DMA_ALIGN)
-        ws_raw = [sb.tile([P, M], U8, name="ws_raw%d" % u, align_bytes=DMA_ALIGN) for u in range(2)]
-        ws = [sb.tile([P, M], U8, name="ws%d" % u, align_bytes=64) for u in range(2)]
+        ws_raw = sb.tile([P, M], U8, name="ws_raw", align_bytes=DMA_ALIGN)
+        ws = sb.tile([P, M], U8, name="ws", align_bytes=64)
         w_codes = sb.tile([P, 2 * M], U8, name="w_codes", align_bytes=64)
         res = [sb.tile([P, SLOTS, N], F32, name="res%d" % g, align_bytes=DMA_ALIGN) for g in range(G)]
         y = [sb.tile([P, SLOTS, N], F32, name="y%d" % g, align_bytes=DMA_ALIGN) for g in range(G)]
         acc = [[ps.tile([P, N_TILE], F32, name="acc%d_%d" % (g, h)) for h in range(SLOTS)] for g in range(G)]
 
-        nc.sync.dma_start(
-            out=x_raw[:].rearrange("p j n -> p (j n)"),
-            in_=x.rearrange("g (p j) n -> (g p) (j n)", j=PACK),
-        )
-        for tile in ws_raw:
-            nc.vector.memset(tile[:].bitcast(I32), 0)
-        w_rows = w_words.rearrange("g p b -> (g p) b").bitcast(I32)
-        for first, end in WORD_PARTS:
-            nc.sync.dma_start(out=w_raw[first:end, :].bitcast(I32), in_=w_rows[first:end, :])
-
-        def load_scales(g):
+        x_rows = x.rearrange("g (p j) n -> (g p) (j n)", j=PACK)
+        x_flat = x_raw[:].rearrange("p j n -> p (j n)")
+        for first in (0, 2 * N):
+            nc.sync.dma_start(out=x_flat[:, first : first + 2 * N], in_=x_rows[:, first : first + 2 * N])
+        nc.vector.memset(ws_raw[:].bitcast(I32), 0)
+        nc.sync.dma_start(out=w_raw[:].bitcast(I32), in_=w_words.rearrange("g p b -> (g p) b").bitcast(I32))
+        for f in range(SCALE_ROWS - 1):
+            nc.sync.dma_start(out=ws_raw[f:P:ROWS, :].bitcast(I32), in_=w_scales[:, f, :].bitcast(I32))
+        f = SCALE_ROWS - 1
+        for g in range(2):
             nc.sync.dma_start(
-                out=ws_raw[g // (G - 1)][ROWS * g : ROWS * g + SCALE_ROWS, :].bitcast(I32),
-                in_=w_scales[g].bitcast(I32),
+                out=ws_raw[ROWS * g + f : P : 2 * ROWS, :].bitcast(I32), in_=w_scales[g:G:2, f, :].bitcast(I32)
             )
-
-        def load_residual(g):
+        for g in range(G):
             nc.sync.dma_start(
                 out=res[g][:].rearrange("p h n -> p (h n)"),
                 in_=r[g].rearrange("(b a h) n -> a b (h n)", b=SPREAD, h=SLOTS),
             )
 
-        for g in range(G - 1):
-            load_scales(g)
-        load_residual(0)
-        load_scales(G - 1)
-        for g in range(1, G):
-            load_residual(g)
-
-        def interleave(copy, first, last):
+        def interleave(copy, first, last, places):
             copy(
-                out=x_bf[:, first:last, :].rearrange("p (c i) j -> p c j i", i=4),
-                in_=x_raw[:, :, first:last].rearrange("p j (c i) -> p c j i", i=4),
+                out=x_bf[:, first:last, places].rearrange("p (c i) j -> p c j i", i=4),
+                in_=x_raw[:, places, first:last].rearrange("p j (c i) -> p c j i", i=4),
             )
 
         def quantize(t):
@@ -95,7 +84,7 @@ def tile_rows_glin_relu_res_kernel(tc, x, w_words, w_scales, r, out):
             nc.tensor.matmul_mx(
                 out=acc[g][h][:],
                 lhsT=w_codes[rows, 2 * P * h : 2 * P * (h + 1)].bitcast(FP4X4),
-                lhsT_scale=ws[g // (G - 1)][rows, P * h : P * (h + 1)],
+                lhsT_scale=ws[rows, P * h : P * (h + 1)],
                 rhs=x_codes[rows, cols].bitcast(FP8X4),
                 rhs_scale=x_scales[rows, cols],
                 start=True,
@@ -113,19 +102,22 @@ def tile_rows_glin_relu_res_kernel(tc, x, w_words, w_scales, r, out):
                 op1=ALU.add,
             )
 
+        low, high = slice(0, 2), slice(2, 4)
+        interleave(nc.vector.tensor_copy, 0, N_TILE + VECTOR_COLS[1], low)
+        interleave(nc.scalar.copy, N_TILE + VECTOR_COLS[1], N, low)
         for t, share in enumerate(VECTOR_COLS):
             first = t * N_TILE
-            interleave(nc.scalar.copy, first + share, first + N_TILE)
-            interleave(nc.vector.tensor_copy, first, first + share)
+            interleave(nc.scalar.copy, first + share, first + N_TILE, high)
+            interleave(nc.vector.tensor_copy, first, first + share, high)
             if t == 0:
                 nc.vector.tensor_copy(
                     out=w_codes[:].rearrange("p (h a b y) -> p h a b y", h=SLOTS, b=SPREAD, y=2),
                     in_=w_raw[:].rearrange("p (b a h y) -> p h a b y", h=SLOTS, b=SPREAD, y=2),
                 )
-            nc.vector.tensor_copy(
-                out=ws[t][:].rearrange("p (h a b) -> p h a b", h=SLOTS, b=SPREAD),
-                in_=ws_raw[t][:].rearrange("p (b a h) -> p h a b", h=SLOTS, b=SPREAD),
-            )
+                nc.vector.tensor_copy(
+                    out=ws[:].rearrange("p (h a b) -> p h a b", h=SLOTS, b=SPREAD),
+                    in_=ws_raw[:].rearrange("p (b a h) -> p h a b", h=SLOTS, b=SPREAD),
+                )
             quantize(t)
 
         def store(g):
@@ -134,29 +126,18 @@ def tile_rows_glin_relu_res_kernel(tc, x, w_words, w_scales, r, out):
                 in_=y[g][:].rearrange("p h n -> p (h n)"),
             )
 
-        last = G - 1
-        order = [(0, 0, 0)]
-        for g in range(last):
-            order.append((g, 1, 0))
-            if g + 1 < last:
-                order.append((g + 1, 0, 0))
-            else:
-                order.append((last, 1, 0))
-            order.extend([(g, 0, 1), (g, 1, 1)])
-        order.extend([(last, 0, 1), (last, 1, 1)])
-
-        multiply(*order[0])
-        multiply(*order[1])
-        multiply(last, 0, 0)
-        nc.scalar.activation(out=y[last][:, 0, 0:N_TILE], in_=acc[last][0][:], func=ACT.Relu)
-        for i, (g, h, t) in enumerate(order):
-            finish(g, h, t)
-            if i + 2 < len(order):
-                multiply(*order[i + 2])
-            if (h, t) == (1, 1) and g < last:
-                store(g)
-            if (g, h, t) == (last - 1, 1, 1):
-                nc.vector.tensor_tensor(
-                    out=y[last][:, 0, 0:N_TILE], in0=y[last][:, 0, 0:N_TILE], in1=res[last][:, 0, 0:N_TILE], op=ALU.add
-                )
-        store(last)
+        for h in range(SLOTS):
+            multiply(0, h, 0)
+        for g in range(G):
+            early = y[g][:, :, 0:N_TILE]
+            for h in range(SLOTS):
+                nc.scalar.activation(out=early[:, h, :], in_=acc[g][h][:], func=ACT.Relu)
+            if g + 1 < G:
+                for h in range(SLOTS):
+                    multiply(g + 1, h, 0)
+            for h in range(SLOTS):
+                multiply(g, h, 1)
+            nc.vector.tensor_tensor(out=early, in0=early, in1=res[g][:, :, 0:N_TILE], op=ALU.add)
+            for h in range(SLOTS):
+                finish(g, h, 1)
+            store(g)

from contextlib import ExitStack

import concourse.mybir as mybir

G, D, M, N = 4, 128, 256, 1024
FLOPS = 2 * G * D * M * N

F32 = mybir.dt.float32
BF16 = mybir.dt.bfloat16
I32 = mybir.dt.int32
U32 = mybir.dt.uint32
U8 = mybir.dt.uint8
FP8X4 = mybir.dt.float8_e4m3fn_x4
FP4X4 = mybir.dt.float4_e2m1fn_x4
ALU = mybir.AluOpType
ACT = mybir.ActivationFunctionType

P = 128
PACK = 4
ROWS = D // PACK
SCALE_ROWS = D // 32
SLOTS = M // P
N_TILE = 512
VECTOR_COLS = (320, 128)
DMA_ALIGN = 256
SPREAD = 4


def tile_rows_glin_relu_res_kernel(tc, x, w_words, w_scales, r, out):
    nc = tc.nc
    with ExitStack() as ctx:
        sb = ctx.enter_context(tc.tile_pool(name="sb", bufs=1))
        ps = ctx.enter_context(tc.psum_pool(name="ps", bufs=1))
        ctx.enter_context(tc.manual_schedule())

        x_raw = sb.tile([P, PACK, N], F32, name="x_raw", align_bytes=DMA_ALIGN)
        x_bf = sb.tile([P, N, PACK], BF16, name="x_bf", align_bytes=64)
        x_codes = sb.tile([P, N], U32, name="x_codes", align_bytes=64)
        x_scales = sb.tile([P, N], U8, name="x_scales", align_bytes=64)
        w_raw = sb.tile([P, 2 * M], U8, name="w_raw", align_bytes=DMA_ALIGN)
        ws_raw = sb.tile([P, M], U8, name="ws_raw", align_bytes=DMA_ALIGN)
        ws = sb.tile([P, M], U8, name="ws", align_bytes=64)
        w_codes = sb.tile([P, 2 * M], U8, name="w_codes", align_bytes=64)
        res = [sb.tile([P, SLOTS, N], F32, name="res%d" % g, align_bytes=DMA_ALIGN) for g in range(G)]
        y = [sb.tile([P, SLOTS, N], F32, name="y%d" % g, align_bytes=DMA_ALIGN) for g in range(G)]
        acc = [[ps.tile([P, N_TILE], F32, name="acc%d_%d" % (g, h)) for h in range(SLOTS)] for g in range(G)]

        x_rows = x.rearrange("g (p j) n -> (g p) (j n)", j=PACK)
        x_flat = x_raw[:].rearrange("p j n -> p (j n)")
        for first in (0, 2 * N):
            nc.sync.dma_start(out=x_flat[:, first : first + 2 * N], in_=x_rows[:, first : first + 2 * N])
        nc.vector.memset(ws_raw[:].bitcast(I32), 0)
        nc.sync.dma_start(out=w_raw[:].bitcast(I32), in_=w_words.rearrange("g p b -> (g p) b").bitcast(I32))
        for f in range(SCALE_ROWS - 1):
            nc.sync.dma_start(out=ws_raw[f:P:ROWS, :].bitcast(I32), in_=w_scales[:, f, :].bitcast(I32))
        f = SCALE_ROWS - 1
        for g in range(2):
            nc.sync.dma_start(
                out=ws_raw[ROWS * g + f : P : 2 * ROWS, :].bitcast(I32), in_=w_scales[g:G:2, f, :].bitcast(I32)
            )
        for g in range(G):
            nc.sync.dma_start(
                out=res[g][:].rearrange("p h n -> p (h n)"),
                in_=r[g].rearrange("(b a h) n -> a b (h n)", b=SPREAD, h=SLOTS),
            )

        def interleave(copy, first, last, places):
            copy(
                out=x_bf[:, first:last, places].rearrange("p (c i) j -> p c j i", i=4),
                in_=x_raw[:, places, first:last].rearrange("p j (c i) -> p c j i", i=4),
            )

        def quantize(t):
            cols = slice(t * N_TILE, (t + 1) * N_TILE)
            nc.vector.quantize_mx(
                out=x_codes[:, cols].bitcast(FP8X4),
                scales=x_scales[:, cols],
                in_=x_bf[:, cols, :].rearrange("p n j -> p (n j)"),
            )

        def multiply(g, h, t):
            rows = slice(ROWS * g, ROWS * (g + 1))
            cols = slice(t * N_TILE, (t + 1) * N_TILE)
            nc.tensor.matmul_mx(
                out=acc[g][h][:],
                lhsT=w_codes[rows, 2 * P * h : 2 * P * (h + 1)].bitcast(FP4X4),
                lhsT_scale=ws[rows, P * h : P * (h + 1)],
                rhs=x_codes[rows, cols].bitcast(FP8X4),
                rhs_scale=x_scales[rows, cols],
                start=True,
                stop=True,
            )

        def finish(g, h, t):
            cols = slice(t * N_TILE, (t + 1) * N_TILE)
            nc.vector.scalar_tensor_tensor(
                out=y[g][:, h, cols],
                in0=acc[g][h][:],
                scalar=0.0,
                in1=res[g][:, h, cols],
                op0=ALU.max,
                op1=ALU.add,
            )

        low, high = slice(0, 2), slice(2, 4)
        interleave(nc.vector.tensor_copy, 0, N_TILE + VECTOR_COLS[1], low)
        interleave(nc.scalar.copy, N_TILE + VECTOR_COLS[1], N, low)
        for t, share in enumerate(VECTOR_COLS):
            first = t * N_TILE
            interleave(nc.scalar.copy, first + share, first + N_TILE, high)
            interleave(nc.vector.tensor_copy, first, first + share, high)
            if t == 0:
                nc.vector.tensor_copy(
                    out=w_codes[:].rearrange("p (h a b y) -> p h a b y", h=SLOTS, b=SPREAD, y=2),
                    in_=w_raw[:].rearrange("p (b a h y) -> p h a b y", h=SLOTS, b=SPREAD, y=2),
                )
                nc.vector.tensor_copy(
                    out=ws[:].rearrange("p (h a b) -> p h a b", h=SLOTS, b=SPREAD),
                    in_=ws_raw[:].rearrange("p (b a h) -> p h a b", h=SLOTS, b=SPREAD),
                )
            quantize(t)

        def store(g):
            nc.sync.dma_start(
                out=out[g].rearrange("(b a h) n -> a b (h n)", b=SPREAD, h=SLOTS),
                in_=y[g][:].rearrange("p h n -> p (h n)"),
            )

        for h in range(SLOTS):
            multiply(0, h, 0)
        for g in range(G):
            early = y[g][:, :, 0:N_TILE]
            for h in range(SLOTS):
                nc.scalar.activation(out=early[:, h, :], in_=acc[g][h][:], func=ACT.Relu)
            if g + 1 < G:
                for h in range(SLOTS):
                    multiply(g + 1, h, 0)
            for h in range(SLOTS):
                multiply(g, h, 1)
            nc.vector.tensor_tensor(out=early, in0=early, in1=res[g][:, :, 0:N_TILE], op=ALU.add)
            for h in range(SLOTS):
                finish(g, h, 1)
            store(g)
